import numpy as np
import ml_dtypes


def mxq(x, axis, fmt="e4m3"):
    dtype, down = {"e4m3": (ml_dtypes.float8_e4m3fn, 7), "e5m2": (ml_dtypes.float8_e5m2, 14)}[fmt]
    v = np.moveaxis(np.asarray(x, np.float32).astype(ml_dtypes.bfloat16).astype(np.float64), axis, -1)
    blocks = v.reshape(v.shape[:-1] + (-1, 32))
    amax = np.abs(blocks).max(-1, keepdims=True)
    byte = np.maximum(np.where(amax > 0, np.frexp(amax)[1] - 1 + 127, 0) - down, 1)
    scale = np.exp2(byte - 127.0)
    codes = (blocks / scale).astype(np.float32).astype(dtype).astype(np.float64)
    return np.moveaxis((codes * scale).reshape(v.shape), -1, axis)


WIDE = False


def mx_kscale(k):
    if not WIDE:
        return np.ones(k)
    levels = np.array([10, -10, 5, -5, 0])
    if k % 512:
        return np.exp2(np.random.permutation(np.resize(levels, k // 32))).repeat(32)
    a = np.empty((k // 512, 16))
    for p in range(k // 512):
        a[p, :8] = np.random.permutation(np.resize(levels, 8))
        for g in range(8):
            far = levels[np.abs(levels - a[p, g]) >= 10]
            a[p, g + 8] = far[np.random.randint(len(far))]
    return np.exp2(a.ravel()).repeat(32)


def f64(x):
    return np.asarray(x).astype(np.float64)


def striped(idx):
    return np.tile(idx.reshape(-1, 16).T, (8, 1)).astype(np.uint16)


def unstriped(offs):
    return offs[:16].T.reshape(-1).astype(np.int64)


def pack_weight(w):
    k, n = w.shape
    w = f64(np.asarray(w, np.float32).astype(ml_dtypes.bfloat16)).reshape(k // 32, 32, n)
    amax = np.abs(w).max(1)
    byte = np.clip(np.where(amax > 0, np.frexp(amax)[1] - 1 + 127 - 7, 1), 1, 254)
    scaled = (w * np.exp2(127.0 - byte)[:, None, :]).reshape(k, n).astype(np.float32)
    words = np.ascontiguousarray(scaled.reshape(k // 512, 128, 4, n).transpose(0, 1, 3, 2)).astype(ml_dtypes.float8_e4m3fn).view(np.uint8)
    return words, np.ascontiguousarray(byte.astype(np.uint8).reshape(k // 512, 16, n))


def unpack_weight(words, scales):
    g, p, n, _ = words.shape
    vals = np.ascontiguousarray(words).view(ml_dtypes.float8_e4m3fn).astype(np.float64) * np.repeat(np.exp2(scales.astype(np.float64) - 127.0), 8, axis=1)[..., None]
    return vals.transpose(0, 1, 3, 2).reshape(g * 512, n)


E2M1 = np.array([0.0, 0.5, 1.0, 1.5, 2.0, 3.0, 4.0, 6.0, -0.0, -0.5, -1.0, -1.5, -2.0, -3.0, -4.0, -6.0])


def pack_fp4(w):
    k, n = w.shape
    w = f64(np.asarray(w, np.float32).astype(ml_dtypes.bfloat16)).reshape(k // 32, 32, n)
    amax = np.abs(w).max(1)
    mant, ex = np.frexp(amax / 6.0)
    byte = np.clip(np.where(amax > 0, np.where(mant > 0.5, ex, ex - 1) + 127, 1), 1, 254)
    scaled = (w * np.exp2(127.0 - byte)[:, None, :]).reshape(k, n).astype(np.float32)
    c = np.ascontiguousarray(scaled.reshape(k // 512, 128, 4, n).transpose(0, 1, 3, 2)).astype(ml_dtypes.float4_e2m1fn).view(np.uint8) & 0xF
    words = (c[..., 0::2] | (c[..., 1::2] << 4)).reshape(k // 512, 128, 2 * n)
    return np.ascontiguousarray(words), np.ascontiguousarray(byte.astype(np.uint8).reshape(k // 512, 16, n))


def unpack_fp4(words, scales):
    g, _, n = scales.shape
    words = np.ascontiguousarray(words).reshape(g, 128, n, 2)
    nib = np.empty((g, 128, n, 4), np.uint8)
    nib[..., 0::2] = words & 0xF
    nib[..., 1::2] = words >> 4
    vals = E2M1[nib] * np.repeat(np.exp2(scales.astype(np.float64) - 127.0), 8, axis=1)[..., None]
    return vals.transpose(0, 1, 3, 2).reshape(g * 512, n)


def relu(v):
    return np.maximum(v, 0.0)


K, T, H, N = 1024, 512, 512, 256


def setup_inputs():
    n = np.random.standard_normal
    s = mx_kscale(K)[:, None]
    u = mx_kscale(H)
    packed_xT = pack_weight(n((K, T)) * s)
    packed_w2 = pack_fp4(n((H, N)) / np.sqrt(2 * H) / u[:, None])
    packed_w3 = pack_fp4(n((H, N)) / np.sqrt(2 * H) / u[:, None])
    return {
        "x_words": packed_xT[0],
        "x_scales": packed_xT[1],
        "w1": (n((K, H)) / np.sqrt(K) / s * u).astype(np.float32),
        "w2_words": packed_w2[0],
        "w2_scales": packed_w2[1],
        "w3_words": packed_w3[0],
        "w3_scales": packed_w3[1],
        "pos1": striped(np.random.permutation(T)),
        "pos2": striped(np.random.permutation(T)),
        "pos3": striped(np.random.permutation(T)),
        "pos4": striped(np.random.permutation(T)),
    }


def reference(x_words, x_scales, w1, w2_words, w2_scales, w3_words, w3_scales, pos1, pos2, pos3, pos4):
    xq = unpack_weight(x_words, x_scales)
    h = relu(mxq(f64(w1), 0, "e4m3").T @ xq)
    z = (h[:, unstriped(pos1)] + h[:, unstriped(pos2)] + h[:, unstriped(pos3)] + h[:, unstriped(pos4)]) / 4
    return unpack_fp4(w2_words, w2_scales).T @ mxq(h, 0, "e4m3") + unpack_fp4(w3_words, w3_scales).T @ mxq(z, 0, "e4m3")

@@ -1,0 +1,257 @@
+from contextlib import ExitStack
+
+import concourse.mybir as mybir
+from concourse.masks import make_identity
+
+K, T, H, N = 1024, 512, 512, 256
+FLOPS = 2 * K * H * T + 2 * 2 * H * N * T
+
+F32 = mybir.dt.float32
+BF16 = mybir.dt.bfloat16
+I32 = mybir.dt.int32
+U32 = mybir.dt.uint32
+U16 = mybir.dt.uint16
+U8 = mybir.dt.uint8
+FP8X4 = mybir.dt.float8_e4m3fn_x4
+FP4X4 = mybir.dt.float4_e2m1fn_x4
+ACT = mybir.ActivationFunctionType
+ALU = mybir.AluOpType
+
+P = 128
+PACK = 4
+K_PASS = P * PACK
+PASSES = K // K_PASS
+BLOCKS = H // P
+CHUNKS = T // P
+LISTS = 4
+WINDOW = 704
+
+
+def tile_picked_wsagecat_mean_l_kernel(
+    tc, x_words, x_scales, w1, w2_words, w2_scales, w3_words, w3_scales, pos1, pos2, pos3, pos4, out
+):
+    nc = tc.nc
+    with ExitStack() as ctx:
+        keep = ctx.enter_context(tc.tile_pool(name="keep", bufs=1))
+        zbanks = ctx.enter_context(tc.psum_pool(name="zbanks", bufs=1))
+        acc = ctx.enter_context(tc.psum_pool(name="acc", bufs=2))
+        turn = ctx.enter_context(tc.psum_pool(name="turn", bufs=2))
+
+        x_planes = keep.tile([P, PASSES, T], U8, name="x_planes", align_bytes=64)
+        nc.gpsimd.memset(x_planes[:].bitcast(I32), 0)
+        w1_raw = [[keep.tile([P, PACK, P], F32, name="w1_raw%d%d" % (b, g), align_bytes=64) for g in range(PASSES)] for b in range(BLOCKS)]
+        x_codes = [keep.tile([P, T], U32, name="x_codes%d" % g, align_bytes=64) for g in range(PASSES)]
+        lists = [keep.tile([P, T // 16], U16, name="list%d" % d) for d in range(LISTS)]
+
+        def load_w1(b):
+            for g in range(PASSES):
+                rows = w1[g * K_PASS : (g + 1) * K_PASS, b * P : (b + 1) * P]
+                nc.sync.dma_start(out=w1_raw[b][g][:], in_=rows.rearrange("(p j) c -> p j c", j=PACK))
+
+        load_w1(0)
+        for q in range(4):
+            nc.scalar.dma_start(
+                out=x_planes[32 * q : 32 * q + 4, :, :].bitcast(I32),
+                in_=x_scales[:, 4 * q : 4 * q + 4, :].rearrange("z r c -> r z c").bitcast(I32),
+            )
+        for g in range(PASSES):
+            nc.sync.dma_start(out=x_codes[g][:].bitcast(I32), in_=x_words[g].rearrange("p c r -> p (c r)").bitcast(I32))
+        nc.sync.dma_start(lists[0][:], pos1)
+        load_w1(1)
+        for d, pos in ((1, pos2), (2, pos3), (3, pos4)):
+            nc.sync.dma_start(lists[d][:], pos)
+        load_w1(2)
+        load_w1(3)
+
+        ident = keep.tile([P, P], F32, name="ident")
+        make_identity(nc, ident[:])
+        h = [keep.tile([P, WINDOW if b < BLOCKS - 1 else T], F32, name="h%d" % b) for b in range(BLOCKS)]
+        for b in range(BLOCKS - 1):
+            nc.gpsimd.memset(h[b][:, T:], 0.0)
+        w23_planes = keep.tile([P, 2, N], U8, name="w23_planes", align_bytes=64)
+        nc.gpsimd.memset(w23_planes[:].bitcast(I32), 0)
+        w23_codes = []
+        for s, (words, scales) in enumerate(((w2_words, w2_scales), (w3_words, w3_scales))):
+            codes = keep.tile([P, 2 * N], U8, name="w23_codes%d" % s, align_bytes=64)
+            nc.sync.dma_start(out=codes[:].bitcast(I32), in_=words[0].bitcast(I32))
+            w23_codes.append(codes)
+        for s, (words, scales) in enumerate(((w2_words, w2_scales), (w3_words, w3_scales))):
+            for q in range(4):
+                nc.sync.dma_start(
+                    out=w23_planes[32 * q : 32 * q + 4, s, :].bitcast(I32),
+                    in_=scales[0, 4 * q : 4 * q + 4, :].bitcast(I32),
+                )
+
+        w1_codes = [keep.tile([P, PASSES, P], U32, name="w1_codes%d" % b, align_bytes=64) for b in range(BLOCKS)]
+        w1_planes = [keep.tile([P, PASSES, P], U8, name="w1_planes%d" % b, align_bytes=64) for b in range(BLOCKS)]
+
+        def cast_w1(b, g, grouped, copy):
+            copy(out=grouped, in_=w1_raw[b][g][:].rearrange("p j c -> p c j"))
+
+        def product1(b):
+            bank = acc.tile([P, T], F32, name="acc")
+            for g in range(PASSES):
+                nc.tensor.matmul_mx(
+                    out=bank[:],
+                    lhsT=w1_codes[b][:, g, :].bitcast(FP8X4),
+                    lhsT_scale=w1_planes[b][:, g, :],
+                    rhs=x_codes[g][:].bitcast(FP8X4),
+                    rhs_scale=x_planes[:, g, :],
+                    start=(g == 0),
+                    stop=(g == PASSES - 1),
+                )
+            return bank
+
+        hT = keep.tile([P, CHUNKS, 2, P, 2], BF16, name="hT", align_bytes=64)
+        zT = [keep.tile([P, 2, P, 2], BF16, name="zT%d" % c, align_bytes=64) for c in range(CHUNKS)]
+
+        def turn_h(b):
+            bank = turn.tile([P, CHUNKS, P], F32, name="turn")
+            for c in range(CHUNKS):
+                nc.tensor.transpose(bank[:, c, :], h[b][:, c * P : (c + 1) * P], ident[:])
+            for u in range(2):
+                nc.scalar.copy(
+                    out=hT[:, :, u, 32 * b : 32 * (b + 1), :],
+                    in_=bank[:].rearrange("v c (p u e) -> v c u p e", u=2, e=2)[:, :, u, :, :],
+                )
+
+        def later_block(b):
+            grouped = keep.tile([P, PASSES, P, PACK], BF16, name="grouped%d" % b, tag="reuse%d" % b, align_bytes=64)
+            for g in range(PASSES):
+                cast_w1(b, g, grouped[:, g, :, :], nc.scalar.copy)
+            nc.vector.quantize_mx(
+                out=w1_codes[b][:].rearrange("p g c -> p (g c)").bitcast(FP8X4),
+                scales=w1_planes[b][:].rearrange("p g c -> p (g c)"),
+                in_=grouped[:].rearrange("p g c j -> p (g c j)"),
+            )
+            bank = product1(b)
+            nc.scalar.activation(out=h[b][:, :T], in_=bank[:], func=ACT.Relu)
+            turn_h(b)
+
+        for g in range(PASSES):
+            grouped = keep.tile([P, P, PACK], BF16, name="grouped0%d" % g, align_bytes=64)
+            cast_w1(0, g, grouped[:], nc.vector.tensor_copy)
+            nc.vector.quantize_mx(
+                out=w1_codes[0][:, g, :].bitcast(FP8X4),
+                scales=w1_planes[0][:, g, :],
+                in_=grouped[:].rearrange("p c j -> p (c j)"),
+            )
+        bank = product1(0)
+        nc.vector.tensor_scalar(out=h[0][:, :T], in0=bank[:], scalar1=0.0, scalar2=None, op0=ALU.max)
+        turn_h(0)
+
+        zbank = [zbanks.tile([P, BLOCKS, P], F32, name="zbank%d" % c) for c in range(CHUNKS)]
+
+        def z_out(b, c):
+            nc.scalar.activation(
+                out=zT[c][:, :, 32 * b : 32 * (b + 1), :],
+                in_=zbank[c][:, b, :].rearrange("v (p u e) -> v u p e", u=2, e=2),
+                func=ACT.Copy,
+                scale=1.0 / LISTS,
+            )
+
+        h_codes = keep.tile([P, T], U32, name="h_codes", align_bytes=64)
+        h_planes = keep.tile([P, T], U8, name="h_planes", align_bytes=64)
+
+        def quantize_h():
+            grouped = keep.tile([P, T, PACK], BF16, name="h_grouped", tag="reuse_h", align_bytes=64)
+            words = grouped[:].rearrange("p v j -> p (v j)").bitcast(F32).rearrange("p (c v u) -> p c v u", c=CHUNKS, u=2)
+            for half in range(2):
+                bank = turn.tile([P, 2, 2, P], F32, name="turn")
+                for c in range(2):
+                    for u in range(2):
+                        src = hT[:, 2 * half + c, u, :, :].rearrange("v p e -> v (p e)").bitcast(F32)
+                        nc.tensor.transpose(bank[:, c, u, :], src, ident[:])
+                nc.scalar.copy(out=words[:, 2 * half : 2 * half + 2, :, :], in_=bank[:].rearrange("p c u v -> p c v u"))
+            nc.vector.quantize_mx(out=h_codes[:].bitcast(FP8X4), scales=h_planes[:], in_=grouped[:].rearrange("p v j -> p (v j)"))
+
+        def gather(b, d, picked):
+            nc.vector.tensor_copy(picked, h[b][:].indirect(lists[d][:]))
+            for c in range(CHUNKS):
+                nc.tensor.matmul(
+                    zbank[c][:, b, :], picked[:, c * P : (c + 1) * P], ident[:],
+                    is_transpose=True, start=(d == 0), stop=(d == LISTS - 1),
+                )
+            if d == LISTS - 1:
+                for c in range(CHUNKS):
+                    z_out(b, c)
+
+        def staging(count, width, tag):
+            return keep.tile([P, count, width], F32, name="picked_" + tag, tag=tag, align_bytes=64)
+
+        picked = staging(1, T, "first")
+        gather(0, 0, picked[:, 0, :])
+        later_block(1)
+        picked = staging(3, T, "reuse1")
+        for d in range(1, LISTS):
+            gather(0, d, picked[:, d - 1, :])
+        later_block(2)
+        picked = staging(1, T, "reuse2")
+        gather(1, 0, picked[:, 0, :])
+        later_block(3)
+        picked = staging(3, T, "reuse3")
+        for d in range(1, LISTS):
+            gather(1, d, picked[:, d - 1, :])
+        quantize_h()
+        picked = staging(2, T, "w1_raw31")
+        for d in range(2):
+            gather(2, d, picked[:, d, :])
+        picked = staging(2, T, "hT")
+        for d in range(2, LISTS):
+            gather(2, d, picked[:, d - 2, :])
+
+        out_view = out.rearrange("(m p) v -> p m v", p=P)
+
+        def turn_back(c):
+            bank = turn.tile([P, 2, P], F32, name="turn")
+            for u in range(2):
+                nc.tensor.transpose(bank[:, u, :], zT[c][:, u, :, :].rearrange("v p e -> v (p e)").bitcast(F32), ident[:])
+            grouped = keep.tile([P, P, PACK], BF16, name="z_grouped", tag="reuse_z%d" % c, align_bytes=64)
+            words = grouped[:].rearrange("p v j -> p (v j)").bitcast(F32).rearrange("p (v u) -> p v u", u=2)
+            nc.scalar.copy(out=words, in_=bank[:].rearrange("p u v -> p v u"))
+            return grouped
+
+        def finish(c, grouped):
+            z_codes = keep.tile([P, P], U32, name="z_codes%d" % c, align_bytes=64)
+            z_planes = keep.tile([P, P], U8, name="z_planes%d" % c, align_bytes=64)
+            nc.vector.quantize_mx(out=z_codes[:].bitcast(FP8X4), scales=z_planes[:], in_=grouped[:].rearrange("p v j -> p (v j)"))
+            cols = slice(c * P, (c + 1) * P)
+            bank = acc.tile([P, 2, P], F32, name="acc")
+            for m in range(2):
+                moving = ((h_codes[:, cols], h_planes[:, cols]), (z_codes[:], z_planes[:]))
+                for s, (codes, planes) in enumerate(moving):
+                    nc.tensor.matmul_mx(
+                        out=bank[:, m, :],
+                        lhsT=w23_codes[s][:, 2 * P * m : 2 * P * (m + 1)].bitcast(FP4X4),
+                        lhsT_scale=w23_planes[:, s, P * m : P * (m + 1)],
+                        rhs=codes.bitcast(FP8X4),
+                        rhs_scale=planes,
+                        start=(s == 0),
+                        stop=(s == 1),
+                    )
+            result = keep.tile([P, 2, P], F32, name="result%d" % c)
+            nc.scalar.copy(out=result[:], in_=bank[:])
+            nc.sync.dma_start(out=out_view[:, :, cols], in_=result[:])
+
+        b = BLOCKS - 1
+        staged = {}
+        main = staging(CHUNKS * LISTS, P, "reuse_h")
+        for c in range(CHUNKS):
+            for d in range(LISTS):
+                picked = main[:, c * LISTS + d, :]
+                if c >= 2 and d == 1:
+                    picked = staging(1, P, "zT%d" % (c - 2))[:, 0, :]
+                if (c, d) == (3, 2):
+                    finish(0, staged[0])
+                    late = staging(2, P, "reuse_z0")
+                if c == 3 and d >= 2:
+                    picked = late[:, d - 2, :]
+                nc.vector.tensor_copy(picked, h[b][:].indirect(lists[d][:, 8 * c : 8 * (c + 1)]))
+                nc.tensor.matmul(
+                    zbank[c][:, b, :], picked, ident[:],
+                    is_transpose=True, start=(d == 0), stop=(d == LISTS - 1),
+                )
+            z_out(b, c)
+            staged[c] = turn_back(c)
+        for c in range(1, CHUNKS):
+            finish(c, staged[c])

@@ -1,7 +1,6 @@
 from contextlib import ExitStack
 
 import concourse.mybir as mybir
-from concourse.masks import make_identity
 
 K, T, H, N = 1024, 512, 512, 256
 FLOPS = 2 * K * H * T + 2 * 2 * H * N * T
@@ -21,10 +20,9 @@ P = 128
 PACK = 4
 K_PASS = P * PACK
 PASSES = K // K_PASS
-BLOCKS = H // P
 CHUNKS = T // P
 LISTS = 4
-WINDOW = 704
+HALF = T // 2
 
 
 def tile_picked_wsagecat_mean_l_kernel(
@@ -33,195 +31,166 @@ def tile_picked_wsagecat_mean_l_kernel(
     nc = tc.nc
     with ExitStack() as ctx:
         keep = ctx.enter_context(tc.tile_pool(name="keep", bufs=1))
-        zbanks = ctx.enter_context(tc.psum_pool(name="zbanks", bufs=1))
-        acc = ctx.enter_context(tc.psum_pool(name="acc", bufs=2))
-        turn = ctx.enter_context(tc.psum_pool(name="turn", bufs=2))
+        psum = ctx.enter_context(tc.psum_pool(name="psum", bufs=1))
 
         x_planes = keep.tile([P, PASSES, T], U8, name="x_planes", align_bytes=64)
-        nc.gpsimd.memset(x_planes[:].bitcast(I32), 0)
-        w1_raw = [[keep.tile([P, PACK, P], F32, name="w1_raw%d%d" % (b, g), align_bytes=64) for g in range(PASSES)] for b in range(BLOCKS)]
-        x_codes = [keep.tile([P, T], U32, name="x_codes%d" % g, align_bytes=64) for g in range(PASSES)]
-        lists = [keep.tile([P, T // 16], U16, name="list%d" % d) for d in range(LISTS)]
+        nc.vector.memset(x_planes[:].bitcast(I32), 0)
+        w23_planes = keep.tile([P, 2, N], U8, name="w23_planes", align_bytes=64)
+        nc.vector.memset(w23_planes[:].bitcast(I32), 0)
 
-        def load_w1(b):
-            for g in range(PASSES):
-                rows = w1[g * K_PASS : (g + 1) * K_PASS, b * P : (b + 1) * P]
-                nc.sync.dma_start(out=w1_raw[b][g][:], in_=rows.rearrange("(p j) c -> p j c", j=PACK))
+        w1_raw = [keep.tile([P, PACK, H], F32, name="w1_raw%d" % g) for g in range(PASSES)]
+
+        def load_w1(g):
+            rows = w1[g * K_PASS : (g + 1) * K_PASS, :]
+            nc.sync.dma_start(out=w1_raw[g][:], in_=rows.rearrange("(p j) c -> p j c", j=PACK))
 
         load_w1(0)
         for q in range(4):
-            nc.scalar.dma_start(
+            nc.sync.dma_start(
                 out=x_planes[32 * q : 32 * q + 4, :, :].bitcast(I32),
                 in_=x_scales[:, 4 * q : 4 * q + 4, :].rearrange("z r c -> r z c").bitcast(I32),
             )
+        load_w1(1)
+        x_codes = [keep.tile([P, T], U32, name="x_codes%d" % g, align_bytes=64) for g in range(PASSES)]
         for g in range(PASSES):
             nc.sync.dma_start(out=x_codes[g][:].bitcast(I32), in_=x_words[g].rearrange("p c r -> p (c r)").bitcast(I32))
-        nc.sync.dma_start(lists[0][:], pos1)
-        load_w1(1)
-        for d, pos in ((1, pos2), (2, pos3), (3, pos4)):
+        lists = [keep.tile([P, T // 16], U16, name="list%d" % d) for d in range(LISTS)]
+        for d, pos in enumerate((pos1, pos2, pos3, pos4)):
             nc.sync.dma_start(lists[d][:], pos)
-        load_w1(2)
-        load_w1(3)
-
-        ident = keep.tile([P, P], F32, name="ident")
-        make_identity(nc, ident[:])
-        h = [keep.tile([P, WINDOW if b < BLOCKS - 1 else T], F32, name="h%d" % b) for b in range(BLOCKS)]
-        for b in range(BLOCKS - 1):
-            nc.gpsimd.memset(h[b][:, T:], 0.0)
-        w23_planes = keep.tile([P, 2, N], U8, name="w23_planes", align_bytes=64)
-        nc.gpsimd.memset(w23_planes[:].bitcast(I32), 0)
         w23_codes = []
-        for s, (words, scales) in enumerate(((w2_words, w2_scales), (w3_words, w3_scales))):
+        for s, words in enumerate((w2_words, w3_words)):
             codes = keep.tile([P, 2 * N], U8, name="w23_codes%d" % s, align_bytes=64)
             nc.sync.dma_start(out=codes[:].bitcast(I32), in_=words[0].bitcast(I32))
             w23_codes.append(codes)
-        for s, (words, scales) in enumerate(((w2_words, w2_scales), (w3_words, w3_scales))):
+        for s, scales in enumerate((w2_scales, w3_scales)):
             for q in range(4):
                 nc.sync.dma_start(
                     out=w23_planes[32 * q : 32 * q + 4, s, :].bitcast(I32),
                     in_=scales[0, 4 * q : 4 * q + 4, :].bitcast(I32),
                 )
 
-        w1_codes = [keep.tile([P, PASSES, P], U32, name="w1_codes%d" % b, align_bytes=64) for b in range(BLOCKS)]
-        w1_planes = [keep.tile([P, PASSES, P], U8, name="w1_planes%d" % b, align_bytes=64) for b in range(BLOCKS)]
+        def quantize(name, grouped, width):
+            codes = keep.tile([P, width], U32, name=name + "_codes", align_bytes=64)
+            planes = keep.tile([P, width], U8, name=name + "_planes", align_bytes=64)
+            nc.vector.quantize_mx(out=codes[:].bitcast(FP8X4), scales=planes[:], in_=grouped.rearrange("p c j -> p (c j)"))
+            return codes, planes
 
-        def cast_w1(b, g, grouped, copy):
-            copy(out=grouped, in_=w1_raw[b][g][:].rearrange("p j c -> p c j"))
+        def w1_slot(g, t):
+            return w1_raw[g][:].rearrange("p j (m t) -> p t m j", t=PACK)[:, t, :, :]
 
-        def product1(b):
-            bank = acc.tile([P, T], F32, name="acc")
-            for g in range(PASSES):
-                nc.tensor.matmul_mx(
-                    out=bank[:],
-                    lhsT=w1_codes[b][:, g, :].bitcast(FP8X4),
-                    lhsT_scale=w1_planes[b][:, g, :],
-                    rhs=x_codes[g][:].bitcast(FP8X4),
-                    rhs_scale=x_planes[:, g, :],
-                    start=(g == 0),
-                    stop=(g == PASSES - 1),
-                )
-            return bank
+        def cast(g, t, copy):
+            grouped = keep.tile([P, P, PACK], BF16, name="w1_grouped", tag="grouped%d%d" % (g, t), align_bytes=64)
+            copy(out=grouped[:], in_=w1_slot(g, t))
+            return grouped
 
-        hT = keep.tile([P, CHUNKS, 2, P, 2], BF16, name="hT", align_bytes=64)
-        zT = [keep.tile([P, 2, P, 2], BF16, name="zT%d" % c, align_bytes=64) for c in range(CHUNKS)]
+        weights = [[None] * PASSES for t in range(PACK)]
 
-        def turn_h(b):
-            bank = turn.tile([P, CHUNKS, P], F32, name="turn")
-            for c in range(CHUNKS):
-                nc.tensor.transpose(bank[:, c, :], h[b][:, c * P : (c + 1) * P], ident[:])
-            for u in range(2):
-                nc.scalar.copy(
-                    out=hT[:, :, u, 32 * b : 32 * (b + 1), :],
-                    in_=bank[:].rearrange("v c (p u e) -> v c u p e", u=2, e=2)[:, :, u, :, :],
-                )
+        def quantize_w1(g, t, grouped):
+            codes, planes = quantize("w1_%d%d" % (g, t), grouped[:], P)
+            weights[t][g] = (codes[:], planes[:])
 
-        def later_block(b):
-            grouped = keep.tile([P, PASSES, P, PACK], BF16, name="grouped%d" % b, tag="reuse%d" % b, align_bytes=64)
-            for g in range(PASSES):
-                cast_w1(b, g, grouped[:, g, :, :], nc.scalar.copy)
-            nc.vector.quantize_mx(
-                out=w1_codes[b][:].rearrange("p g c -> p (g c)").bitcast(FP8X4),
-                scales=w1_planes[b][:].rearrange("p g c -> p (g c)"),
-                in_=grouped[:].rearrange("p g c j -> p (g c j)"),
+        def product1(weights, g, cols, target):
+            nc.tensor.matmul_mx(
+                out=target,
+                lhsT=weights[g][0].bitcast(FP8X4),
+                lhsT_scale=weights[g][1],
+                rhs=x_codes[g][:, cols].bitcast(FP8X4),
+                rhs_scale=x_planes[:, g, cols],
+                start=(g == 0),
+                stop=(g == PASSES - 1),
             )
-            bank = product1(b)
-            nc.scalar.activation(out=h[b][:, :T], in_=bank[:], func=ACT.Relu)
-            turn_h(b)
 
+        h = [keep.tile([P, T], F32, name="h%d" % t) for t in range(PACK)]
+        h_rounded = keep.tile([P, PACK, T], BF16, name="h_rounded")
+        halves = (slice(0, HALF), slice(HALF, T))
+
+        for t in (0, 1):
+            quantize_w1(0, t, cast(0, t, nc.vector.tensor_copy))
+        waiting = [cast(0, t, nc.scalar.copy) for t in (2, 3)]
+        quantize_w1(0, 2, waiting[0])
+        quantize_w1(1, 0, cast(1, 0, nc.vector.tensor_copy))
+        quantize_w1(0, 3, waiting[1])
+        banks = [psum.tile([P, HALF], F32, name="pair%d" % a) for a in range(2)]
         for g in range(PASSES):
-            grouped = keep.tile([P, P, PACK], BF16, name="grouped0%d" % g, align_bytes=64)
-            cast_w1(0, g, grouped[:], nc.vector.tensor_copy)
-            nc.vector.quantize_mx(
-                out=w1_codes[0][:, g, :].bitcast(FP8X4),
-                scales=w1_planes[0][:, g, :],
-                in_=grouped[:].rearrange("p c j -> p (c j)"),
-            )
-        bank = product1(0)
-        nc.vector.tensor_scalar(out=h[0][:, :T], in0=bank[:], scalar1=0.0, scalar2=None, op0=ALU.max)
-        turn_h(0)
+            for a in range(2):
+                product1(weights[0], g, halves[a], banks[a][:])
+        for a in range(2):
+            nc.vector.tensor_scalar(out=h[0][:, halves[a]], in0=banks[a][:], scalar1=0.0, scalar2=None, op0=ALU.max)
 
-        zbank = [zbanks.tile([P, BLOCKS, P], F32, name="zbank%d" % c) for c in range(CHUNKS)]
+        def later_slot(t):
+            quantize_w1(1, t, cast(1, t, nc.scalar.copy))
+            bank = psum.tile([P, T], F32, name="first%d" % t)
+            for g in range(PASSES):
+                product1(weights[t], g, slice(0, T), bank[:])
+            nc.scalar.activation(out=h[t][:], in_=bank[:], func=ACT.Relu)
 
-        def z_out(b, c):
-            nc.scalar.activation(
-                out=zT[c][:, :, 32 * b : 32 * (b + 1), :],
-                in_=zbank[c][:, b, :].rearrange("v (p u e) -> v u p e", u=2, e=2),
-                func=ACT.Copy,
-                scale=1.0 / LISTS,
-            )
+        def gather(t, d, cols, target, onto):
+            looked_up = h[t][:].indirect(lists[d][:, cols.start // 16 : cols.stop // 16])
+            if d == 0:
+                nc.vector.tensor_copy(target, looked_up)
+            else:
+                nc.vector.tensor_tensor(target, looked_up, onto, ALU.add)
 
-        h_codes = keep.tile([P, T], U32, name="h_codes", align_bytes=64)
-        h_planes = keep.tile([P, T], U8, name="h_planes", align_bytes=64)
+        def staging(tag):
+            return keep.tile([P, T], F32, name="sum_" + tag, tag=tag, align_bytes=64)
 
-        def quantize_h():
-            grouped = keep.tile([P, T, PACK], BF16, name="h_grouped", tag="reuse_h", align_bytes=64)
-            words = grouped[:].rearrange("p v j -> p (v j)").bitcast(F32).rearrange("p (c v u) -> p c v u", c=CHUNKS, u=2)
-            for half in range(2):
-                bank = turn.tile([P, 2, 2, P], F32, name="turn")
-                for c in range(2):
-                    for u in range(2):
-                        src = hT[:, 2 * half + c, u, :, :].rearrange("v p e -> v (p e)").bitcast(F32)
-                        nc.tensor.transpose(bank[:, c, u, :], src, ident[:])
-                nc.scalar.copy(out=words[:, 2 * half : 2 * half + 2, :, :], in_=bank[:].rearrange("p c u v -> p c v u"))
-            nc.vector.quantize_mx(out=h_codes[:].bitcast(FP8X4), scales=h_planes[:], in_=grouped[:].rearrange("p v j -> p (v j)"))
+        def step(t, d, target, onto):
+            for cols in halves:
+                gather(t, d, cols, target[:, cols], None if d == 0 else onto[:, cols])
+            return target
 
-        def gather(b, d, picked):
-            nc.vector.tensor_copy(picked, h[b][:].indirect(lists[d][:]))
-            for c in range(CHUNKS):
-                nc.tensor.matmul(
-                    zbank[c][:, b, :], picked[:, c * P : (c + 1) * P], ident[:],
-                    is_transpose=True, start=(d == 0), stop=(d == LISTS - 1),
-                )
-            if d == LISTS - 1:
-                for c in range(CHUNKS):
-                    z_out(b, c)
+        sums = step(0, 0, staging("s00"), None)
+        later_slot(1)
+        sums = step(0, 1, staging("grouped11"), sums)
+        sums = step(0, 2, staging("s02"), sums)
+        later_slot(2)
+        z = keep.tile([P, PACK, T], F32, name="z", tag="grouped12", align_bytes=64)
+        step(0, 3, z[:, 0, :], sums)
+        sums = step(1, 0, staging("s10"), None)
+        later_slot(3)
+        sums = step(1, 1, staging("grouped13"), sums)
+        sums = step(1, 2, staging("s12"), sums)
+        step(1, 3, z[:, 1, :], sums)
 
-        def staging(count, width, tag):
-            return keep.tile([P, count, width], F32, name="picked_" + tag, tag=tag, align_bytes=64)
+        for t in range(PACK):
+            nc.scalar.copy(out=h_rounded[:, t, :], in_=h[t][:])
+        h_grouped = []
+        for a in range(2):
+            grouped = keep.tile([P, HALF, PACK], BF16, name="h_grouped", tag="reuse_h%d" % a, align_bytes=64)
+            nc.scalar.copy(out=grouped[:], in_=h_rounded[:, :, halves[a]].rearrange("p t v -> p v t"))
+            h_grouped.append(grouped)
 
-        picked = staging(1, T, "first")
-        gather(0, 0, picked[:, 0, :])
-        later_block(1)
-        picked = staging(3, T, "reuse1")
-        for d in range(1, LISTS):
-            gather(0, d, picked[:, d - 1, :])
-        later_block(2)
-        picked = staging(1, T, "reuse2")
-        gather(1, 0, picked[:, 0, :])
-        later_block(3)
-        picked = staging(3, T, "reuse3")
-        for d in range(1, LISTS):
-            gather(1, d, picked[:, d - 1, :])
-        quantize_h()
-        picked = staging(2, T, "w1_raw31")
-        for d in range(2):
-            gather(2, d, picked[:, d, :])
-        picked = staging(2, T, "hT")
-        for d in range(2, LISTS):
-            gather(2, d, picked[:, d - 2, :])
+        sums = None
+        for d in range(LISTS - 1):
+            sums = step(2, d, staging("s2%d" % d), sums)
+        step(2, 3, z[:, 2, :], sums)
+        h_quantized = [quantize("h0", h_grouped[0][:], HALF)]
 
         out_view = out.rearrange("(m p) v -> p m v", p=P)
+        chunks = [slice(c * P, (c + 1) * P) for c in range(CHUNKS)]
 
-        def turn_back(c):
-            bank = turn.tile([P, 2, P], F32, name="turn")
-            for u in range(2):
-                nc.tensor.transpose(bank[:, u, :], zT[c][:, u, :, :].rearrange("v p e -> v (p e)").bitcast(F32), ident[:])
+        def group_z(c):
             grouped = keep.tile([P, P, PACK], BF16, name="z_grouped", tag="reuse_z%d" % c, align_bytes=64)
-            words = grouped[:].rearrange("p v j -> p (v j)").bitcast(F32).rearrange("p (v u) -> p v u", u=2)
-            nc.scalar.copy(out=words, in_=bank[:].rearrange("p u v -> p v u"))
+            nc.scalar.activation(
+                out=grouped[:], in_=z[:, :, chunks[c]].rearrange("p t v -> p v t"), func=ACT.Copy, scale=1.0 / LISTS
+            )
             return grouped
 
         def finish(c, grouped):
-            z_codes = keep.tile([P, P], U32, name="z_codes%d" % c, align_bytes=64)
-            z_planes = keep.tile([P, P], U8, name="z_planes%d" % c, align_bytes=64)
-            nc.vector.quantize_mx(out=z_codes[:].bitcast(FP8X4), scales=z_planes[:], in_=grouped[:].rearrange("p v j -> p (v j)"))
-            cols = slice(c * P, (c + 1) * P)
-            bank = acc.tile([P, 2, P], F32, name="acc")
+            z_codes, z_planes = quantize("z%d" % c, grouped[:], P)
+            cols = chunks[c]
+            h_codes, h_planes = h_quantized[c // 2]
+            last = c == CHUNKS - 1
+            if last:
+                targets = [psum.tile([P, P], F32, name="pair%d" % m)[:] for m in range(2)]
+            else:
+                bank = psum.tile([P, 2, P], F32, name="second%d" % c)
+                targets = [bank[:, m, :] for m in range(2)]
             for m in range(2):
-                moving = ((h_codes[:, cols], h_planes[:, cols]), (z_codes[:], z_planes[:]))
+                moving = ((h_codes[:, chunks[c % 2]], h_planes[:, chunks[c % 2]]), (z_codes[:], z_planes[:]))
                 for s, (codes, planes) in enumerate(moving):
                     nc.tensor.matmul_mx(
-                        out=bank[:, m, :],
+                        out=targets[m],
                         lhsT=w23_codes[s][:, 2 * P * m : 2 * P * (m + 1)].bitcast(FP4X4),
                         lhsT_scale=w23_planes[:, s, P * m : P * (m + 1)],
                         rhs=codes.bitcast(FP8X4),
@@ -230,28 +199,34 @@ def tile_picked_wsagecat_mean_l_kernel(
                         stop=(s == 1),
                     )
             result = keep.tile([P, 2, P], F32, name="result%d" % c)
-            nc.scalar.copy(out=result[:], in_=bank[:])
+            if last:
+                nc.vector.tensor_copy(out=result[:, 0, :], in_=targets[0])
+                nc.scalar.copy(out=result[:, 1, :], in_=targets[1])
+            else:
+                nc.scalar.copy(out=result[:], in_=bank[:])
             nc.sync.dma_start(out=out_view[:, :, cols], in_=result[:])
 
-        b = BLOCKS - 1
-        staged = {}
-        main = staging(CHUNKS * LISTS, P, "reuse_h")
-        for c in range(CHUNKS):
-            for d in range(LISTS):
-                picked = main[:, c * LISTS + d, :]
-                if c >= 2 and d == 1:
-                    picked = staging(1, P, "zT%d" % (c - 2))[:, 0, :]
-                if (c, d) == (3, 2):
-                    finish(0, staged[0])
-                    late = staging(2, P, "reuse_z0")
-                if c == 3 and d >= 2:
-                    picked = late[:, d - 2, :]
-                nc.vector.tensor_copy(picked, h[b][:].indirect(lists[d][:, 8 * c : 8 * (c + 1)]))
-                nc.tensor.matmul(
-                    zbank[c][:, b, :], picked, ident[:],
-                    is_transpose=True, start=(d == 0), stop=(d == LISTS - 1),
-                )
-            z_out(b, c)
-            staged[c] = turn_back(c)
-        for c in range(1, CHUNKS):
+        steps = keep.tile([P, LISTS - 1, T], F32, name="last_sums", tag="reuse_h0", align_bytes=64)
+        wide, third, fourth = halves[0], chunks[2], chunks[3]
+        held = {}
+
+        def last_step(d, cols, target=None):
+            if target is None:
+                target = z[:, 3, cols] if d == LISTS - 1 else steps[:, d, cols]
+            gather(3, d, cols, target, held.get(cols.start))
+            held[cols.start] = target
+
+        for d, cols in ((0, wide), (0, third), (1, wide), (1, third), (2, wide), (0, fourth), (3, wide)):
+            last_step(d, cols)
+        staged = [group_z(0), group_z(1)]
+        for d, cols in ((2, third), (1, fourth), (3, third)):
+            last_step(d, cols)
+        staged.append(group_z(2))
+        finish(0, staged[0])
+        last_step(2, fourth, keep.tile([P, P], F32, name="late", tag="reuse_z0", align_bytes=64)[:])
+        last_step(3, fourth)
+        staged.append(group_z(3))
+        finish(1, staged[1])
+        h_quantized.append(quantize("h1", h_grouped[1][:], HALF))
+        for c in (2, 3):
             finish(c, staged[c])

@@ -20,9 +20,16 @@ P = 128
 PACK = 4
 K_PASS = P * PACK
 PASSES = K // K_PASS
-CHUNKS = T // P
+QUADRANTS = 4
 LISTS = 4
+PER_COLUMN = 16
 HALF = T // 2
+CHUNKS = T // P
+ROW_TILES = N // P
+LAST_SLOT = PACK - 1
+LAST_LIST = LISTS - 1
+WIDE_WINDOW = 704
+ALIGN = 64
 
 
 def tile_picked_wsagecat_mean_l_kernel(
@@ -33,9 +40,9 @@ def tile_picked_wsagecat_mean_l_kernel(
         keep = ctx.enter_context(tc.tile_pool(name="keep", bufs=1))
         psum = ctx.enter_context(tc.psum_pool(name="psum", bufs=1))
 
-        x_planes = keep.tile([P, PASSES, T], U8, name="x_planes", align_bytes=64)
+        x_planes = keep.tile([P, PASSES, T], U8, name="x_planes", align_bytes=ALIGN)
         nc.vector.memset(x_planes[:].bitcast(I32), 0)
-        w23_planes = keep.tile([P, 2, N], U8, name="w23_planes", align_bytes=64)
+        w23_planes = keep.tile([P, 2, N], U8, name="w23_planes", align_bytes=ALIGN)
         nc.vector.memset(w23_planes[:].bitcast(I32), 0)
 
         w1_raw = [keep.tile([P, PACK, H], F32, name="w1_raw%d" % g) for g in range(PASSES)]
@@ -45,149 +52,165 @@ def tile_picked_wsagecat_mean_l_kernel(
             nc.sync.dma_start(out=w1_raw[g][:], in_=rows.rearrange("(p j) c -> p j c", j=PACK))
 
         load_w1(0)
-        for q in range(4):
+        for q in range(QUADRANTS):
             nc.sync.dma_start(
                 out=x_planes[32 * q : 32 * q + 4, :, :].bitcast(I32),
-                in_=x_scales[:, 4 * q : 4 * q + 4, :].rearrange("z r c -> r z c").bitcast(I32),
+                in_=x_scales[:, 4 * q : 4 * q + 4, :].rearrange("g r c -> r g c").bitcast(I32),
             )
         load_w1(1)
-        x_codes = [keep.tile([P, T], U32, name="x_codes%d" % g, align_bytes=64) for g in range(PASSES)]
+        x_codes = [keep.tile([P, T], U32, name="x_codes%d" % g, align_bytes=ALIGN) for g in range(PASSES)]
         for g in range(PASSES):
             nc.sync.dma_start(out=x_codes[g][:].bitcast(I32), in_=x_words[g].rearrange("p c r -> p (c r)").bitcast(I32))
-        lists = [keep.tile([P, T // 16], U16, name="list%d" % d) for d in range(LISTS)]
+        lists = [keep.tile([P, T // PER_COLUMN], U16, name="list%d" % d) for d in range(LISTS)]
         for d, pos in enumerate((pos1, pos2, pos3, pos4)):
             nc.sync.dma_start(lists[d][:], pos)
+
         w23_codes = []
         for s, words in enumerate((w2_words, w3_words)):
-            codes = keep.tile([P, 2 * N], U8, name="w23_codes%d" % s, align_bytes=64)
+            codes = keep.tile([P, 2 * N], U8, name="w23_codes%d" % s, align_bytes=ALIGN)
             nc.sync.dma_start(out=codes[:].bitcast(I32), in_=words[0].bitcast(I32))
             w23_codes.append(codes)
         for s, scales in enumerate((w2_scales, w3_scales)):
-            for q in range(4):
+            for q in range(QUADRANTS):
                 nc.sync.dma_start(
                     out=w23_planes[32 * q : 32 * q + 4, s, :].bitcast(I32),
                     in_=scales[0, 4 * q : 4 * q + 4, :].bitcast(I32),
                 )
 
         def quantize(name, grouped, width):
-            codes = keep.tile([P, width], U32, name=name + "_codes", align_bytes=64)
-            planes = keep.tile([P, width], U8, name=name + "_planes", align_bytes=64)
-            nc.vector.quantize_mx(out=codes[:].bitcast(FP8X4), scales=planes[:], in_=grouped.rearrange("p c j -> p (c j)"))
+            codes = keep.tile([P, width], U32, name=name + "_codes", align_bytes=ALIGN)
+            planes = keep.tile([P, width], U8, name=name + "_planes", align_bytes=ALIGN)
+            nc.vector.quantize_mx(
+                out=codes[:].bitcast(FP8X4), scales=planes[:], in_=grouped[:].rearrange("p c j -> p (c j)")
+            )
             return codes, planes
 
-        def w1_slot(g, t):
-            return w1_raw[g][:].rearrange("p j (m t) -> p t m j", t=PACK)[:, t, :, :]
-
-        def cast(g, t, copy):
-            grouped = keep.tile([P, P, PACK], BF16, name="w1_grouped", tag="grouped%d%d" % (g, t), align_bytes=64)
-            copy(out=grouped[:], in_=w1_slot(g, t))
+        def group_w1(g, t, copy):
+            grouped = keep.tile([P, P, PACK], BF16, name="w1_grouped", tag="w1_grouped%d%d" % (g, t), align_bytes=ALIGN)
+            copy(out=grouped[:], in_=w1_raw[g][:].rearrange("p j (m t) -> p t m j", t=PACK)[:, t, :, :])
             return grouped
 
-        weights = [[None] * PASSES for t in range(PACK)]
+        w1_quantized = {}
 
         def quantize_w1(g, t, grouped):
-            codes, planes = quantize("w1_%d%d" % (g, t), grouped[:], P)
-            weights[t][g] = (codes[:], planes[:])
+            w1_quantized[g, t] = quantize("w1_%d%d" % (g, t), grouped, P)
 
-        def product1(weights, g, cols, target):
+        def first_product(g, t, cols, target):
+            codes, planes = w1_quantized[g, t]
             nc.tensor.matmul_mx(
                 out=target,
-                lhsT=weights[g][0].bitcast(FP8X4),
-                lhsT_scale=weights[g][1],
+                lhsT=codes[:].bitcast(FP8X4),
+                lhsT_scale=planes[:],
                 rhs=x_codes[g][:, cols].bitcast(FP8X4),
                 rhs_scale=x_planes[:, g, cols],
                 start=(g == 0),
                 stop=(g == PASSES - 1),
             )
 
-        h = [keep.tile([P, T], F32, name="h%d" % t) for t in range(PACK)]
-        h_rounded = keep.tile([P, PACK, T], BF16, name="h_rounded")
+        h = [keep.tile([P, T if t == LAST_SLOT else WIDE_WINDOW], F32, name="h%d" % t) for t in range(PACK)]
+        for t in range(LAST_SLOT):
+            nc.vector.memset(h[t][:, T:], 0.0)
+        zero = {t: keep.tile([P, 1], F32, name="zero%d" % t, align_bytes=ALIGN) for t in range(1, PACK)}
+        for t in range(1, PACK):
+            nc.vector.memset(zero[t][:], 0.0)
+        h_rounded = keep.tile([P, PACK, T], BF16, name="h_rounded", align_bytes=ALIGN)
+        whole = slice(0, T)
         halves = (slice(0, HALF), slice(HALF, T))
+        chunks = [slice(c * P, (c + 1) * P) for c in range(CHUNKS)]
 
         for t in (0, 1):
-            quantize_w1(0, t, cast(0, t, nc.vector.tensor_copy))
-        waiting = [cast(0, t, nc.scalar.copy) for t in (2, 3)]
-        quantize_w1(0, 2, waiting[0])
-        quantize_w1(1, 0, cast(1, 0, nc.vector.tensor_copy))
-        quantize_w1(0, 3, waiting[1])
-        banks = [psum.tile([P, HALF], F32, name="pair%d" % a) for a in range(2)]
+            quantize_w1(0, t, group_w1(0, t, nc.vector.tensor_copy))
+        by_scalar = {t: group_w1(0, t, nc.scalar.copy) for t in (2, 3)}
+        quantize_w1(0, 2, by_scalar[2])
+        quantize_w1(1, 0, group_w1(1, 0, nc.vector.tensor_copy))
+        quantize_w1(0, 3, by_scalar[3])
+
+        half_banks = [psum.tile([P, HALF], F32, name="pair%d" % a) for a in range(2)]
         for g in range(PASSES):
             for a in range(2):
-                product1(weights[0], g, halves[a], banks[a][:])
+                first_product(g, 0, halves[a], half_banks[a][:])
+        quantize_w1(1, 1, group_w1(1, 1, nc.scalar.copy))
         for a in range(2):
-            nc.vector.tensor_scalar(out=h[0][:, halves[a]], in0=banks[a][:], scalar1=0.0, scalar2=None, op0=ALU.max)
+            nc.vector.tensor_scalar(
+                out=h[0][:, halves[a]], in0=half_banks[a][:], scalar1=0.0, scalar2=None, op0=ALU.max
+            )
 
         def later_slot(t):
-            quantize_w1(1, t, cast(1, t, nc.scalar.copy))
             bank = psum.tile([P, T], F32, name="first%d" % t)
             for g in range(PASSES):
-                product1(weights[t], g, slice(0, T), bank[:])
-            nc.scalar.activation(out=h[t][:], in_=bank[:], func=ACT.Relu)
+                first_product(g, t, whole, bank[:])
+            nc.scalar.activation(out=h[t][:, whole], in_=bank[:], func=ACT.Relu, bias=zero[t][:])
 
         def gather(t, d, cols, target, onto):
-            looked_up = h[t][:].indirect(lists[d][:, cols.start // 16 : cols.stop // 16])
+            looked_up = h[t][:].indirect(lists[d][:, cols.start // PER_COLUMN : cols.stop // PER_COLUMN])
             if d == 0:
                 nc.vector.tensor_copy(target, looked_up)
             else:
                 nc.vector.tensor_tensor(target, looked_up, onto, ALU.add)
 
-        def staging(tag):
-            return keep.tile([P, T], F32, name="sum_" + tag, tag=tag, align_bytes=64)
+        def sum_tile(tag):
+            return keep.tile([P, T], F32, name="sum_" + tag, tag=tag, align_bytes=ALIGN)
 
-        def step(t, d, target, onto):
+        z = keep.tile([P, PACK, T], F32, name="z")
+        sums = {}
+
+        def step_in_halves(t, d, tag):
+            target = sum_tile(tag)
             for cols in halves:
-                gather(t, d, cols, target[:, cols], None if d == 0 else onto[:, cols])
-            return target
+                gather(t, d, cols, target[:, cols], sums[t][:, cols] if d > 0 else None)
+            sums[t] = target[:]
 
-        sums = step(0, 0, staging("s00"), None)
+        def step(t, d, tag=None):
+            target = z[:, t, :] if d == LAST_LIST else sum_tile(tag or "sum%d%d" % (t, d))[:]
+            gather(t, d, whole, target, sums.get(t))
+            sums[t] = target
+
         later_slot(1)
-        sums = step(0, 1, staging("grouped11"), sums)
-        sums = step(0, 2, staging("s02"), sums)
+        step_in_halves(0, 0, "sum00")
+        quantize_w1(1, 2, group_w1(1, 2, nc.scalar.copy))
         later_slot(2)
-        z = keep.tile([P, PACK, T], F32, name="z", tag="grouped12", align_bytes=64)
-        step(0, 3, z[:, 0, :], sums)
-        sums = step(1, 0, staging("s10"), None)
+        step_in_halves(0, 1, "w1_grouped12")
+        quantize_w1(1, 3, group_w1(1, 3, nc.scalar.copy))
         later_slot(3)
-        sums = step(1, 1, staging("grouped13"), sums)
-        sums = step(1, 2, staging("s12"), sums)
-        step(1, 3, z[:, 1, :], sums)
+        step(1, 0, "w1_grouped13")
+        step(0, 2, "zero1")
+        step(1, 1)
+        step(0, 3)
+        step(1, 2, "zero2")
+        step(2, 0)
+        step(1, 3)
+        step(2, 1, "zero3")
 
         for t in range(PACK):
-            nc.scalar.copy(out=h_rounded[:, t, :], in_=h[t][:])
+            nc.scalar.copy(out=h_rounded[:, t, :], in_=h[t][:, whole])
         h_grouped = []
         for a in range(2):
-            grouped = keep.tile([P, HALF, PACK], BF16, name="h_grouped", tag="reuse_h%d" % a, align_bytes=64)
+            grouped = keep.tile([P, HALF, PACK], BF16, name="h_grouped", tag="h_grouped%d" % a, align_bytes=ALIGN)
             nc.scalar.copy(out=grouped[:], in_=h_rounded[:, :, halves[a]].rearrange("p t v -> p v t"))
             h_grouped.append(grouped)
-
-        sums = None
-        for d in range(LISTS - 1):
-            sums = step(2, d, staging("s2%d" % d), sums)
-        step(2, 3, z[:, 2, :], sums)
-        h_quantized = [quantize("h0", h_grouped[0][:], HALF)]
+        h_quantized = [quantize("h0", h_grouped[0], HALF)]
 
         out_view = out.rearrange("(m p) v -> p m v", p=P)
-        chunks = [slice(c * P, (c + 1) * P) for c in range(CHUNKS)]
 
         def group_z(c):
-            grouped = keep.tile([P, P, PACK], BF16, name="z_grouped", tag="reuse_z%d" % c, align_bytes=64)
+            grouped = keep.tile([P, P, PACK], BF16, name="z_grouped", tag="z_grouped%d" % c, align_bytes=ALIGN)
             nc.scalar.activation(
                 out=grouped[:], in_=z[:, :, chunks[c]].rearrange("p t v -> p v t"), func=ACT.Copy, scale=1.0 / LISTS
             )
             return grouped
 
-        def finish(c, grouped):
-            z_codes, z_planes = quantize("z%d" % c, grouped[:], P)
-            cols = chunks[c]
+        def second_product(c, z_grouped):
+            z_codes, z_planes = quantize("z%d" % c, z_grouped, P)
             h_codes, h_planes = h_quantized[c // 2]
+            in_half = chunks[c % 2]
             last = c == CHUNKS - 1
             if last:
-                targets = [psum.tile([P, P], F32, name="pair%d" % m)[:] for m in range(2)]
+                targets = [psum.tile([P, P], F32, name="pair%d" % m)[:] for m in range(ROW_TILES)]
             else:
-                bank = psum.tile([P, 2, P], F32, name="second%d" % c)
-                targets = [bank[:, m, :] for m in range(2)]
-            for m in range(2):
-                moving = ((h_codes[:, chunks[c % 2]], h_planes[:, chunks[c % 2]]), (z_codes[:], z_planes[:]))
+                bank = psum.tile([P, ROW_TILES, P], F32, name="second%d" % c)
+                targets = [bank[:, m, :] for m in range(ROW_TILES)]
+            for m in range(ROW_TILES):
+                moving = ((h_codes[:, in_half], h_planes[:, in_half]), (z_codes[:], z_planes[:]))
                 for s, (codes, planes) in enumerate(moving):
                     nc.tensor.matmul_mx(
                         out=targets[m],
@@ -198,35 +221,39 @@ def tile_picked_wsagecat_mean_l_kernel(
                         start=(s == 0),
                         stop=(s == 1),
                     )
-            result = keep.tile([P, 2, P], F32, name="result%d" % c)
+            result = keep.tile([P, ROW_TILES, P], F32, name="result%d" % c)
             if last:
                 nc.vector.tensor_copy(out=result[:, 0, :], in_=targets[0])
                 nc.scalar.copy(out=result[:, 1, :], in_=targets[1])
             else:
                 nc.scalar.copy(out=result[:], in_=bank[:])
-            nc.sync.dma_start(out=out_view[:, :, cols], in_=result[:])
+            nc.sync.dma_start(out=out_view[:, :, chunks[c]], in_=result[:])
 
-        steps = keep.tile([P, LISTS - 1, T], F32, name="last_sums", tag="reuse_h0", align_bytes=64)
-        wide, third, fourth = halves[0], chunks[2], chunks[3]
-        held = {}
+        last_sums = keep.tile([P, LAST_LIST, T], F32, name="last_sums", tag="h_grouped0", align_bytes=ALIGN)
+        front, third, fourth = halves[0], chunks[2], chunks[3]
+        range_sums = {}
 
         def last_step(d, cols, target=None):
             if target is None:
-                target = z[:, 3, cols] if d == LISTS - 1 else steps[:, d, cols]
-            gather(3, d, cols, target, held.get(cols.start))
-            held[cols.start] = target
+                target = z[:, LAST_SLOT, cols] if d == LAST_LIST else last_sums[:, d, cols]
+            gather(LAST_SLOT, d, cols, target, range_sums.get(cols.start))
+            range_sums[cols.start] = target
 
-        for d, cols in ((0, wide), (0, third), (1, wide), (1, third), (2, wide), (0, fourth), (3, wide)):
+        last_step(0, front)
+        step(2, 2, "h_rounded")
+        last_step(0, third)
+        step(2, 3)
+        for d, cols in ((1, front), (1, third), (2, front), (0, fourth), (3, front)):
             last_step(d, cols)
-        staged = [group_z(0), group_z(1)]
+        z_grouped = [group_z(0), group_z(1)]
         for d, cols in ((2, third), (1, fourth), (3, third)):
             last_step(d, cols)
-        staged.append(group_z(2))
-        finish(0, staged[0])
-        last_step(2, fourth, keep.tile([P, P], F32, name="late", tag="reuse_z0", align_bytes=64)[:])
+        z_grouped.append(group_z(2))
+        second_product(0, z_grouped[0])
+        last_step(2, fourth, keep.tile([P, P], F32, name="late_sum", tag="z_grouped0", align_bytes=ALIGN)[:])
         last_step(3, fourth)
-        staged.append(group_z(3))
-        finish(1, staged[1])
-        h_quantized.append(quantize("h1", h_grouped[1][:], HALF))
+        z_grouped.append(group_z(3))
+        second_product(1, z_grouped[1])
+        h_quantized.append(quantize("h1", h_grouped[1], HALF))
         for c in (2, 3):
-            finish(c, staged[c])
+            second_product(c, z_grouped[c])

from contextlib import ExitStack

import concourse.mybir as mybir

K, T, H, N = 1024, 512, 512, 256
FLOPS = 2 * K * H * T + 2 * 2 * H * N * T

F32 = mybir.dt.float32
BF16 = mybir.dt.bfloat16
I32 = mybir.dt.int32
U32 = mybir.dt.uint32
U16 = mybir.dt.uint16
U8 = mybir.dt.uint8
FP8X4 = mybir.dt.float8_e4m3fn_x4
FP4X4 = mybir.dt.float4_e2m1fn_x4
ACT = mybir.ActivationFunctionType
ALU = mybir.AluOpType

P = 128
PACK = 4
K_PASS = P * PACK
PASSES = K // K_PASS
QUADRANTS = 4
LISTS = 4
PER_COLUMN = 16
HALF = T // 2
CHUNKS = T // P
ROW_TILES = N // P
LAST_SLOT = PACK - 1
LAST_LIST = LISTS - 1
WIDE_WINDOW = 704
ALIGN = 64


def tile_picked_wsagecat_mean_l_kernel(
    tc, x_words, x_scales, w1, w2_words, w2_scales, w3_words, w3_scales, pos1, pos2, pos3, pos4, out
):
    nc = tc.nc
    with ExitStack() as ctx:
        keep = ctx.enter_context(tc.tile_pool(name="keep", bufs=1))
        psum = ctx.enter_context(tc.psum_pool(name="psum", bufs=1))

        x_planes = keep.tile([P, PASSES, T], U8, name="x_planes", align_bytes=ALIGN)
        nc.vector.memset(x_planes[:].bitcast(I32), 0)
        w23_planes = keep.tile([P, 2, N], U8, name="w23_planes", align_bytes=ALIGN)
        nc.vector.memset(w23_planes[:].bitcast(I32), 0)

        w1_raw = [keep.tile([P, PACK, H], F32, name="w1_raw%d" % g) for g in range(PASSES)]

        def load_w1(g):
            rows = w1[g * K_PASS : (g + 1) * K_PASS, :]
            nc.sync.dma_start(out=w1_raw[g][:], in_=rows.rearrange("(p j) c -> p j c", j=PACK))

        load_w1(0)
        for q in range(QUADRANTS):
            nc.sync.dma_start(
                out=x_planes[32 * q : 32 * q + 4, :, :].bitcast(I32),
                in_=x_scales[:, 4 * q : 4 * q + 4, :].rearrange("g r c -> r g c").bitcast(I32),
            )
        load_w1(1)
        x_codes = [keep.tile([P, T], U32, name="x_codes%d" % g, align_bytes=ALIGN) for g in range(PASSES)]
        for g in range(PASSES):
            nc.sync.dma_start(out=x_codes[g][:].bitcast(I32), in_=x_words[g].rearrange("p c r -> p (c r)").bitcast(I32))
        lists = [keep.tile([P, T // PER_COLUMN], U16, name="list%d" % d) for d in range(LISTS)]
        for d, pos in enumerate((pos1, pos2, pos3, pos4)):
            nc.sync.dma_start(lists[d][:], pos)

        w23_codes = []
        for s, words in enumerate((w2_words, w3_words)):
            codes = keep.tile([P, 2 * N], U8, name="w23_codes%d" % s, align_bytes=ALIGN)
            nc.sync.dma_start(out=codes[:].bitcast(I32), in_=words[0].bitcast(I32))
            w23_codes.append(codes)
        for s, scales in enumerate((w2_scales, w3_scales)):
            for q in range(QUADRANTS):
                nc.sync.dma_start(
                    out=w23_planes[32 * q : 32 * q + 4, s, :].bitcast(I32),
                    in_=scales[0, 4 * q : 4 * q + 4, :].bitcast(I32),
                )

        def quantize(name, grouped, width):
            codes = keep.tile([P, width], U32, name=name + "_codes", align_bytes=ALIGN)
            planes = keep.tile([P, width], U8, name=name + "_planes", align_bytes=ALIGN)
            nc.vector.quantize_mx(
                out=codes[:].bitcast(FP8X4), scales=planes[:], in_=grouped[:].rearrange("p c j -> p (c j)")
            )
            return codes, planes

        def group_w1(g, t, copy):
            grouped = keep.tile([P, P, PACK], BF16, name="w1_grouped", tag="w1_grouped%d%d" % (g, t), align_bytes=ALIGN)
            copy(out=grouped[:], in_=w1_raw[g][:].rearrange("p j (m t) -> p t m j", t=PACK)[:, t, :, :])
            return grouped

        w1_quantized = {}

        def quantize_w1(g, t, grouped):
            w1_quantized[g, t] = quantize("w1_%d%d" % (g, t), grouped, P)

        def first_product(g, t, cols, target):
            codes, planes = w1_quantized[g, t]
            nc.tensor.matmul_mx(
                out=target,
                lhsT=codes[:].bitcast(FP8X4),
                lhsT_scale=planes[:],
                rhs=x_codes[g][:, cols].bitcast(FP8X4),
                rhs_scale=x_planes[:, g, cols],
                start=(g == 0),
                stop=(g == PASSES - 1),
            )

        h = [keep.tile([P, T if t == LAST_SLOT else WIDE_WINDOW], F32, name="h%d" % t) for t in range(PACK)]
        for t in range(LAST_SLOT):
            nc.vector.memset(h[t][:, T:], 0.0)
        zero = {t: keep.tile([P, 1], F32, name="zero%d" % t, align_bytes=ALIGN) for t in range(1, PACK)}
        for t in range(1, PACK):
            nc.vector.memset(zero[t][:], 0.0)
        h_rounded = keep.tile([P, PACK, T], BF16, name="h_rounded", align_bytes=ALIGN)
        whole = slice(0, T)
        halves = (slice(0, HALF), slice(HALF, T))
        chunks = [slice(c * P, (c + 1) * P) for c in range(CHUNKS)]

        for t in (0, 1):
            quantize_w1(0, t, group_w1(0, t, nc.vector.tensor_copy))
        by_scalar = {t: group_w1(0, t, nc.scalar.copy) for t in (2, 3)}
        quantize_w1(0, 2, by_scalar[2])
        quantize_w1(1, 0, group_w1(1, 0, nc.vector.tensor_copy))
        quantize_w1(0, 3, by_scalar[3])

        half_banks = [psum.tile([P, HALF], F32, name="pair%d" % a) for a in range(2)]
        for g in range(PASSES):
            for a in range(2):
                first_product(g, 0, halves[a], half_banks[a][:])
        quantize_w1(1, 1, group_w1(1, 1, nc.scalar.copy))
        for a in range(2):
            nc.vector.tensor_scalar(
                out=h[0][:, halves[a]], in0=half_banks[a][:], scalar1=0.0, scalar2=None, op0=ALU.max
            )

        def later_slot(t):
            bank = psum.tile([P, T], F32, name="first%d" % t)
            for g in range(PASSES):
                first_product(g, t, whole, bank[:])
            nc.scalar.activation(out=h[t][:, whole], in_=bank[:], func=ACT.Relu, bias=zero[t][:])

        def gather(t, d, cols, target, onto):
            looked_up = h[t][:].indirect(lists[d][:, cols.start // PER_COLUMN : cols.stop // PER_COLUMN])
            if d == 0:
                nc.vector.tensor_copy(target, looked_up)
            else:
                nc.vector.tensor_tensor(target, looked_up, onto, ALU.add)

        def sum_tile(tag):
            return keep.tile([P, T], F32, name="sum_" + tag, tag=tag, align_bytes=ALIGN)

        z = keep.tile([P, PACK, T], F32, name="z")
        sums = {}

        def step_in_halves(t, d, tag):
            target = sum_tile(tag)
            for cols in halves:
                gather(t, d, cols, target[:, cols], sums[t][:, cols] if d > 0 else None)
            sums[t] = target[:]

        def step(t, d, tag=None):
            target = z[:, t, :] if d == LAST_LIST else sum_tile(tag or "sum%d%d" % (t, d))[:]
            gather(t, d, whole, target, sums.get(t))
            sums[t] = target

        later_slot(1)
        step_in_halves(0, 0, "sum00")
        quantize_w1(1, 2, group_w1(1, 2, nc.scalar.copy))
        later_slot(2)
        step_in_halves(0, 1, "w1_grouped12")
        quantize_w1(1, 3, group_w1(1, 3, nc.scalar.copy))
        later_slot(3)
        step(1, 0, "w1_grouped13")
        step(0, 2, "zero1")
        step(1, 1)
        step(0, 3)
        step(1, 2, "zero2")
        step(2, 0)
        step(1, 3)
        step(2, 1, "zero3")

        for t in range(PACK):
            nc.scalar.copy(out=h_rounded[:, t, :], in_=h[t][:, whole])
        h_grouped = []
        for a in range(2):
            grouped = keep.tile([P, HALF, PACK], BF16, name="h_grouped", tag="h_grouped%d" % a, align_bytes=ALIGN)
            nc.scalar.copy(out=grouped[:], in_=h_rounded[:, :, halves[a]].rearrange("p t v -> p v t"))
            h_grouped.append(grouped)
        h_quantized = [quantize("h0", h_grouped[0], HALF)]

        out_view = out.rearrange("(m p) v -> p m v", p=P)

        def group_z(c):
            grouped = keep.tile([P, P, PACK], BF16, name="z_grouped", tag="z_grouped%d" % c, align_bytes=ALIGN)
            nc.scalar.activation(
                out=grouped[:], in_=z[:, :, chunks[c]].rearrange("p t v -> p v t"), func=ACT.Copy, scale=1.0 / LISTS
            )
            return grouped

        def second_product(c, z_grouped):
            z_codes, z_planes = quantize("z%d" % c, z_grouped, P)
            h_codes, h_planes = h_quantized[c // 2]
            in_half = chunks[c % 2]
            last = c == CHUNKS - 1
            if last:
                targets = [psum.tile([P, P], F32, name="pair%d" % m)[:] for m in range(ROW_TILES)]
            else:
                bank = psum.tile([P, ROW_TILES, P], F32, name="second%d" % c)
                targets = [bank[:, m, :] for m in range(ROW_TILES)]
            for m in range(ROW_TILES):
                moving = ((h_codes[:, in_half], h_planes[:, in_half]), (z_codes[:], z_planes[:]))
                for s, (codes, planes) in enumerate(moving):
                    nc.tensor.matmul_mx(
                        out=targets[m],
                        lhsT=w23_codes[s][:, 2 * P * m : 2 * P * (m + 1)].bitcast(FP4X4),
                        lhsT_scale=w23_planes[:, s, P * m : P * (m + 1)],
                        rhs=codes.bitcast(FP8X4),
                        rhs_scale=planes,
                        start=(s == 0),
                        stop=(s == 1),
                    )
            result = keep.tile([P, ROW_TILES, P], F32, name="result%d" % c)
            if last:
                nc.vector.tensor_copy(out=result[:, 0, :], in_=targets[0])
                nc.scalar.copy(out=result[:, 1, :], in_=targets[1])
            else:
                nc.scalar.copy(out=result[:], in_=bank[:])
            nc.sync.dma_start(out=out_view[:, :, chunks[c]], in_=result[:])

        last_sums = keep.tile([P, LAST_LIST, T], F32, name="last_sums", tag="h_grouped0", align_bytes=ALIGN)
        front, third, fourth = halves[0], chunks[2], chunks[3]
        range_sums = {}

        def last_step(d, cols, target=None):
            if target is None:
                target = z[:, LAST_SLOT, cols] if d == LAST_LIST else last_sums[:, d, cols]
            gather(LAST_SLOT, d, cols, target, range_sums.get(cols.start))
            range_sums[cols.start] = target

        last_step(0, front)
        step(2, 2, "h_rounded")
        last_step(0, third)
        step(2, 3)
        for d, cols in ((1, front), (1, third), (2, front), (0, fourth), (3, front)):
            last_step(d, cols)
        z_grouped = [group_z(0), group_z(1)]
        for d, cols in ((2, third), (1, fourth), (3, third)):
            last_step(d, cols)
        z_grouped.append(group_z(2))
        second_product(0, z_grouped[0])
        last_step(2, fourth, keep.tile([P, P], F32, name="late_sum", tag="z_grouped0", align_bytes=ALIGN)[:])
        last_step(3, fourth)
        z_grouped.append(group_z(3))
        second_product(1, z_grouped[1])
        h_quantized.append(quantize("h1", h_grouped[1], HALF))
        for c in (2, 3):
            second_product(c, z_grouped[c])
